import numpy as np
import ml_dtypes


def mxq(x, axis, fmt="e4m3"):
    dtype, down = {"e4m3": (ml_dtypes.float8_e4m3fn, 7), "e5m2": (ml_dtypes.float8_e5m2, 14)}[fmt]
    v = np.moveaxis(np.asarray(x, np.float32).astype(ml_dtypes.bfloat16).astype(np.float64), axis, -1)
    blocks = v.reshape(v.shape[:-1] + (-1, 32))
    amax = np.abs(blocks).max(-1, keepdims=True)
    byte = np.maximum(np.where(amax > 0, np.frexp(amax)[1] - 1 + 127, 0) - down, 1)
    scale = np.exp2(byte - 127.0)
    codes = (blocks / scale).astype(np.float32).astype(dtype).astype(np.float64)
    return np.moveaxis((codes * scale).reshape(v.shape), -1, axis)


WIDE = False


def mx_kscale(k):
    if not WIDE:
        return np.ones(k)
    levels = np.array([10, -10, 5, -5, 0])
    if k % 512:
        return np.exp2(np.random.permutation(np.resize(levels, k // 32))).repeat(32)
    a = np.empty((k // 512, 16))
    for p in range(k // 512):
        a[p, :8] = np.random.permutation(np.resize(levels, 8))
        for g in range(8):
            far = levels[np.abs(levels - a[p, g]) >= 10]
            a[p, g + 8] = far[np.random.randint(len(far))]
    return np.exp2(a.ravel()).repeat(32)


def f64(x):
    return np.asarray(x).astype(np.float64)


def striped(idx):
    return np.tile(idx.reshape(-1, 16).T, (8, 1)).astype(np.uint16)


def unstriped(offs):
    return offs[:16].T.reshape(-1).astype(np.int64)


def striped8(idx):
    return np.concatenate([x.reshape(-1, 16).T for x in idx]).astype(np.uint16)


def runs(offs, k):
    lists = np.stack([offs[16 * r : 16 * r + 16].T.reshape(-1) for r in range(8)]).astype(np.int64)
    return lists[np.arange(k) % 512 // 64]


def pack_weight(w):
    k, n = w.shape
    w = f64(np.asarray(w, np.float32).astype(ml_dtypes.bfloat16)).reshape(k // 32, 32, n)
    amax = np.abs(w).max(1)
    byte = np.clip(np.where(amax > 0, np.frexp(amax)[1] - 1 + 127 - 7, 1), 1, 254)
    scaled = (w * np.exp2(127.0 - byte)[:, None, :]).reshape(k, n).astype(np.float32)
    words = np.ascontiguousarray(scaled.reshape(k // 512, 128, 4, n).transpose(0, 1, 3, 2)).astype(ml_dtypes.float8_e4m3fn).view(np.uint8)
    return words, np.ascontiguousarray(byte.astype(np.uint8).reshape(k // 512, 16, n))


def unpack_weight(words, scales):
    g, p, n, _ = words.shape
    vals = np.ascontiguousarray(words).view(ml_dtypes.float8_e4m3fn).astype(np.float64) * np.repeat(np.exp2(scales.astype(np.float64) - 127.0), 8, axis=1)[..., None]
    return vals.transpose(0, 1, 3, 2).reshape(g * 512, n)


K, T, S, G, H = 512, 1024, 512, 2048, 512


def setup_inputs():
    n = np.random.standard_normal
    s = mx_kscale(K)[:, None]
    packed_xT = pack_weight(n((K, T)) * s)
    packed_dT = pack_weight(n((K, G)) / s)
    return {
        "x_words": packed_xT[0],
        "x_scales": packed_xT[1],
        "d_words": packed_dT[0],
        "d_scales": packed_dT[1],
        "gs": (np.random.uniform(0.5, 1.5, (K, 1)) * s).astype(np.float32),
        "offs": striped(np.random.permutation(T)[:S]),
        "k1": striped8(np.random.randint(0, G, (8, H))),
        "n1": striped8(np.stack([np.random.permutation(S) for _ in range(8)])),
        "n2": striped8(np.stack([np.random.permutation(S) for _ in range(8)])),
        "k2": striped8(np.random.randint(0, G, (8, H))),
        "n3": striped8(np.stack([np.random.permutation(S) for _ in range(8)])),
        "n4": striped8(np.stack([np.random.permutation(S) for _ in range(8)])),
    }


def reference(x_words, x_scales, d_words, d_scales, gs, offs, k1, n1, n2, k2, n3, n4):
    d_k2 = unpack_weight(d_words, d_scales)[np.arange(K)[:, None], runs(k2, K)]
    d_k1 = unpack_weight(d_words, d_scales)[np.arange(K)[:, None], runs(k1, K)]
    xq = unpack_weight(x_words, x_scales)[:, unstriped(offs)]
    h = 0.0625 * (d_k1.T @ xq)
    z = f64(gs) * (0.75 * (h[np.arange(H)[:, None], runs(n1, H)] + h[np.arange(H)[:, None], runs(n2, H)]) - h)
    h2 = 0.0625 * ((d_k2.T @ mxq(z, 0, "e4m3")))
    return np.minimum(np.maximum(h2, h2[np.arange(H)[:, None], runs(n3, H)]), h2[np.arange(H)[:, None], runs(n4, H)])

@@ -1,0 +1,199 @@
+from contextlib import ExitStack
+
+import concourse.mybir as mybir
+
+F32 = mybir.dt.float32
+BF16 = mybir.dt.bfloat16
+I32 = mybir.dt.int32
+U32 = mybir.dt.uint32
+U16 = mybir.dt.uint16
+U8 = mybir.dt.uint8
+FP8X4 = mybir.dt.float8_e4m3fn_x4
+ALU = mybir.AluOpType
+COPY = mybir.ActivationFunctionType.Copy
+
+P = 128
+K, T, S, G, H = 512, 1024, 512, 2048, 512
+TILES = 4
+HALF = S // 2
+FLOPS = 2 * 2 * K * H * S
+
+
+def tile_picked_codelapminmx_none_p_kernel(
+    tc, x_words, x_scales, d_words, d_scales, gs, offs, k1, n1, n2, k2, n3, n4, out
+):
+    nc = tc.nc
+    with ExitStack() as ctx:
+        lists = ctx.enter_context(tc.tile_pool(name="lists", bufs=1))
+        keep = ctx.enter_context(tc.tile_pool(name="keep", bufs=1))
+        psum = ctx.enter_context(tc.psum_pool(name="psum", bufs=1))
+
+        def load_list(name, dram):
+            tile = lists.tile([P, S // 16], U16, name=name)
+            nc.sync.dma_start(tile[:], dram)
+            return tile
+
+        d_bytes = keep.tile([P, G], U8, name="d_bytes", align_bytes=64)
+        x_bytes = keep.tile([P, T], U8, name="x_bytes", align_bytes=64)
+        d_table = keep.tile([P, G], U32, name="d_table", align_bytes=64)
+        x_table = keep.tile([P, T], U32, name="x_table", align_bytes=64)
+        nc.vector.memset(d_bytes[:].bitcast(I32), 0)
+        nc.vector.memset(x_bytes[:].bitcast(I32), 0)
+
+        k1_list = load_list("k1_list", k1)
+        d_rows = d_scales[0].bitcast(I32)
+        for e in range(2):
+            nc.sync.dma_start(d_bytes[:].bitcast(I32)[e:P:16, :], d_rows[e:16:2, :])
+        nc.scalar.dma_start(d_table[:].bitcast(I32), d_words[0].rearrange("p n t -> p (n t)").bitcast(I32))
+        x_rows = x_scales[0].bitcast(I32)
+        for j in range(4):
+            nc.sync.dma_start(x_bytes[:].bitcast(I32)[j:P:32, :], x_rows[j:16:4, :])
+        offs_list = load_list("offs_list", offs)
+        nc.scalar.dma_start(x_table[:].bitcast(I32), x_words[0].rearrange("p n t -> p (n t)").bitcast(I32))
+        k2_list = load_list("k2_list", k2)
+        n1_list = load_list("n1_list", n1)
+        n2_list = load_list("n2_list", n2)
+        n3_list = load_list("n3_list", n3)
+        n4_list = load_list("n4_list", n4)
+
+        gain = keep.tile([P, TILES], F32, name="gain")
+        nc.gpsimd.dma_start(gain[:], gs.rearrange("(p t) o -> p (t o)", t=TILES))
+        gain_self = keep.tile([P, TILES], F32, name="gain_self")
+        gain_near = keep.tile([P, TILES], F32, name="gain_near")
+        nc.scalar.activation(gain_self[:], gain[:], COPY, scale=0.0625)
+        nc.scalar.activation(gain_near[:], gain[:], COPY, scale=0.0625 * 0.75)
+
+        def lift_odd_rows(plane):
+            rows = plane[:].bitcast(I32)
+            for e in range(2):
+                nc.sync.dma_start(rows[2 + e : P : 32, :], rows[16 + e : P : 32, :])
+
+        w1_bytes_picked = keep.tile([P, H], U8, name="w1_bytes_picked", align_bytes=64)
+        nc.vector.tensor_copy(w1_bytes_picked[:], d_bytes[:].indirect(k1_list[:]))
+        w1_scales = keep.tile([P, H], U8, name="w1_scales", align_bytes=64)
+        nc.vector.tensor_copy(
+            w1_scales[:].rearrange("p (t c i) -> p c t i", t=4, i=16),
+            w1_bytes_picked[:].rearrange("p (c i t) -> p c t i", t=4, i=16),
+        )
+        lift_odd_rows(w1_scales)
+
+        xq_scales = keep.tile([P, S], U8, name="xq_scales", align_bytes=64)
+        nc.vector.tensor_copy(xq_scales[:], x_bytes[:].indirect(offs_list[:]))
+
+        w1_words_picked = keep.tile([P, H], U32, name="w1_words_picked", align_bytes=64)
+        nc.vector.tensor_copy(w1_words_picked[:], d_table[:].indirect(k1_list[:]))
+        w1_words = keep.tile([P, H], U32, name="w1_words", align_bytes=64)
+        nc.vector.tensor_copy(
+            w1_words[:].rearrange("p (t c i) -> p c t i", t=4, i=4),
+            w1_words_picked[:].rearrange("p (c i t) -> p c t i", t=4, i=4),
+        )
+
+        xq_words = keep.tile([P, S], U32, name="xq_words", align_bytes=64)
+        for c in range(2):
+            nc.vector.tensor_copy(
+                xq_words[:, c * HALF : (c + 1) * HALF], x_table[:].indirect(offs_list[:, c * 16 : (c + 1) * 16])
+            )
+
+        w2_bytes_picked = keep.tile([P, H], U8, name="w2_bytes_picked", align_bytes=64)
+        nc.vector.tensor_copy(w2_bytes_picked[:], d_bytes[:].indirect(k2_list[:]))
+        w2_scales = keep.tile([P, H], U8, name="w2_scales", align_bytes=64)
+        nc.vector.tensor_copy(
+            w2_scales[:].bitcast(I32).rearrange("p (t a v) -> p a t v", t=4, v=2),
+            w2_bytes_picked[:].bitcast(I32).rearrange("p (a t v) -> p a t v", t=4, v=2),
+        )
+        lift_odd_rows(w2_scales)
+
+        def product(tag, words, scales, t, rhs_words, rhs_scales, c0, c1):
+            acc = psum.tile([P, c1 - c0], F32, name=tag, tag=tag)
+            nc.tensor.matmul_mx(
+                out=acc[:],
+                lhsT=words[:, t * P : (t + 1) * P].bitcast(FP8X4),
+                lhsT_scale=scales[:, t * P : (t + 1) * P],
+                rhs=rhs_words[:, c0:c1].bitcast(FP8X4),
+                rhs_scale=rhs_scales[:, c0:c1],
+                start=True,
+                stop=True,
+            )
+            return acc
+
+        near = [keep.tile([P, S], F32, name="near%d" % t) for t in range(TILES)]
+        wide = [keep.tile([P, 2 * S], F32, name="wide%d" % t) for t in range(TILES)]
+        late = []
+        for t in range(TILES):
+            spans = [(0, HALF), (HALF, S)] if t == 0 else [(0, S)]
+            for i, (c0, c1) in enumerate(spans):
+                acc = product("bank%d_%d" % (t, i), w1_words, w1_scales, t, xq_words, xq_scales, c0, c1)
+                nc.scalar.activation(near[t][:, c0:c1], acc[:], COPY, scale=gain_near[:, t : t + 1])
+                if c0 == 0:
+                    nc.scalar.activation(wide[t][:, S : S + HALF], acc[:, :HALF], COPY, scale=gain_self[:, t : t + 1])
+                if c1 == S:
+                    late.append((t, acc, HALF - c0))
+        for t, acc, c0 in late:
+            nc.scalar.activation(wide[t][:, S + HALF :], acc[:, c0 : c0 + HALF], COPY, scale=gain_self[:, t : t + 1])
+
+        z_words = keep.tile([P, S], U32, name="z_words", align_bytes=64)
+        z_scales = keep.tile([P, S], U8, name="z_scales", align_bytes=64)
+        z = [keep.tile([P, TILES, HALF], F32, name="z%d" % c) for c in range(2)]
+        grouped = [keep.tile([P, HALF, TILES], BF16, name="grouped%d" % c, align_bytes=64) for c in range(2)]
+        partial = {}
+
+        def first_neighbour(c, t):
+            tag = "shared" if (c, t) == (0, TILES - 1) else "partial%d_%d" % (c, t)
+            partial[c, t] = keep.tile([P, HALF], F32, name="partial%d_%d" % (c, t), tag=tag, align_bytes=64)
+            nc.vector.tensor_tensor(
+                partial[c, t][:],
+                near[t][:].indirect(n1_list[:, c * 16 : (c + 1) * 16]),
+                wide[t][:, S + c * HALF : S + (c + 1) * HALF],
+                ALU.subtract,
+            )
+
+        def second_neighbour(c, t):
+            nc.vector.tensor_tensor(
+                z[c][:, t, :], near[t][:].indirect(n2_list[:, c * 16 : (c + 1) * 16]), partial[c, t][:], ALU.add
+            )
+            if t == TILES - 1:
+                nc.scalar.copy(
+                    grouped[c][:].rearrange("p (b i) t -> p b t i", i=4),
+                    z[c][:].rearrange("p t (b i) -> p b t i", i=4),
+                )
+
+        def quantise(c):
+            nc.vector.quantize_mx(
+                out=z_words[:, c * HALF : (c + 1) * HALF].bitcast(FP8X4),
+                scales=z_scales[:, c * HALF : (c + 1) * HALF],
+                in_=grouped[c][:].rearrange("p s t -> p (s t)"),
+            )
+
+        steps = [(c, t) for c in range(2) for t in range(TILES)]
+        for i, step in enumerate(steps):
+            first_neighbour(*step)
+            if i > 0:
+                second_neighbour(*steps[i - 1])
+        second_neighbour(*steps[-1])
+        quantise(0)
+
+        w2_words_picked = keep.tile([P, H], U32, name="w2_words_picked", tag="shared", align_bytes=64)
+        nc.vector.tensor_copy(w2_words_picked[:], d_table[:].indirect(k2_list[:]))
+        w2_words = keep.tile([P, H], U32, name="w2_words", align_bytes=64)
+        nc.vector.tensor_copy(
+            w2_words[:].rearrange("p (t a v) -> p a t v", t=4, v=8),
+            w2_words_picked[:].rearrange("p (a t v) -> p a t v", t=4, v=8),
+        )
+        quantise(1)
+
+        out_rows = out.rearrange("(a t v) s -> t a v s", t=TILES, v=8)
+        for t in range(TILES):
+            spans = [(0, HALF), (HALF, S)] if t == 0 else [(0, S)]
+            for i, (c0, c1) in enumerate(spans):
+                acc = product("bank%d_%d" % (t, i), w2_words, w2_scales, t, z_words, z_scales, c0, c1)
+                nc.scalar.activation(wide[t][:, c0:c1], acc[:], COPY, scale=0.0625)
+        for t in range(TILES):
+            third = keep.tile([P, S], F32, name="third%d" % t)
+            fourth = keep.tile([P, S], F32, name="fourth%d" % t)
+            larger = keep.tile([P, S], F32, name="larger%d" % t)
+            result = keep.tile([P, S], F32, name="result%d" % t)
+            nc.vector.tensor_copy(third[:], wide[t][:].indirect(n3_list[:]))
+            nc.vector.tensor_copy(fourth[:], wide[t][:].indirect(n4_list[:]))
+            nc.vector.tensor_tensor(larger[:], third[:], wide[t][:, :S], ALU.max)
+            nc.vector.tensor_tensor(result[:], larger[:], fourth[:], ALU.min)
+            nc.sync.dma_start(out_rows[t], result[:])

@@ -42,14 +42,16 @@ def tile_picked_codelapminmx_none_p_kernel(
 
         k1_list = load_list("k1_list", k1)
         d_rows = d_scales[0].bitcast(I32)
+        d_source = d_words[0].rearrange("p n t -> p (n t)").bitcast(I32)
+        nc.sync.dma_start(d_table[:].bitcast(I32)[:, : G // 4], d_source[:, : G // 4])
         for e in range(2):
             nc.sync.dma_start(d_bytes[:].bitcast(I32)[e:P:16, :], d_rows[e:16:2, :])
-        nc.scalar.dma_start(d_table[:].bitcast(I32), d_words[0].rearrange("p n t -> p (n t)").bitcast(I32))
         x_rows = x_scales[0].bitcast(I32)
         for j in range(4):
             nc.sync.dma_start(x_bytes[:].bitcast(I32)[j:P:32, :], x_rows[j:16:4, :])
         offs_list = load_list("offs_list", offs)
-        nc.scalar.dma_start(x_table[:].bitcast(I32), x_words[0].rearrange("p n t -> p (n t)").bitcast(I32))
+        nc.sync.dma_start(d_table[:].bitcast(I32)[:, G // 4 :], d_source[:, G // 4 :])
+        nc.sync.dma_start(x_table[:].bitcast(I32), x_words[0].rearrange("p n t -> p (n t)").bitcast(I32))
         k2_list = load_list("k2_list", k2)
         n1_list = load_list("n1_list", n1)
         n2_list = load_list("n2_list", n2)
@@ -70,6 +72,9 @@ def tile_picked_codelapminmx_none_p_kernel(
 
         w1_bytes_picked = keep.tile([P, H], U8, name="w1_bytes_picked", align_bytes=64)
         nc.vector.tensor_copy(w1_bytes_picked[:], d_bytes[:].indirect(k1_list[:]))
+
+        xq_scales = keep.tile([P, S], U8, name="xq_scales", align_bytes=64)
+        nc.vector.tensor_copy(xq_scales[:], x_bytes[:].indirect(offs_list[:]))
         w1_scales = keep.tile([P, H], U8, name="w1_scales", align_bytes=64)
         nc.vector.tensor_copy(
             w1_scales[:].rearrange("p (t c i) -> p c t i", t=4, i=16),
@@ -77,31 +82,20 @@ def tile_picked_codelapminmx_none_p_kernel(
         )
         lift_odd_rows(w1_scales)
 
-        xq_scales = keep.tile([P, S], U8, name="xq_scales", align_bytes=64)
-        nc.vector.tensor_copy(xq_scales[:], x_bytes[:].indirect(offs_list[:]))
-
         w1_words_picked = keep.tile([P, H], U32, name="w1_words_picked", align_bytes=64)
         nc.vector.tensor_copy(w1_words_picked[:], d_table[:].indirect(k1_list[:]))
+
+        xq_words = keep.tile([P, S], U32, name="xq_words", align_bytes=64)
+        nc.vector.tensor_copy(xq_words[:, :HALF], x_table[:].indirect(offs_list[:, :16]))
         w1_words = keep.tile([P, H], U32, name="w1_words", align_bytes=64)
         nc.vector.tensor_copy(
             w1_words[:].rearrange("p (t c i) -> p c t i", t=4, i=4),
             w1_words_picked[:].rearrange("p (c i t) -> p c t i", t=4, i=4),
         )
-
-        xq_words = keep.tile([P, S], U32, name="xq_words", align_bytes=64)
-        for c in range(2):
-            nc.vector.tensor_copy(
-                xq_words[:, c * HALF : (c + 1) * HALF], x_table[:].indirect(offs_list[:, c * 16 : (c + 1) * 16])
-            )
+        nc.vector.tensor_copy(xq_words[:, HALF:], x_table[:].indirect(offs_list[:, 16:]))
 
         w2_bytes_picked = keep.tile([P, H], U8, name="w2_bytes_picked", align_bytes=64)
         nc.vector.tensor_copy(w2_bytes_picked[:], d_bytes[:].indirect(k2_list[:]))
-        w2_scales = keep.tile([P, H], U8, name="w2_scales", align_bytes=64)
-        nc.vector.tensor_copy(
-            w2_scales[:].bitcast(I32).rearrange("p (t a v) -> p a t v", t=4, v=2),
-            w2_bytes_picked[:].bitcast(I32).rearrange("p (a t v) -> p a t v", t=4, v=2),
-        )
-        lift_odd_rows(w2_scales)
 
         def product(tag, words, scales, t, rhs_words, rhs_scales, c0, c1):
             acc = psum.tile([P, c1 - c0], F32, name=tag, tag=tag)
@@ -165,15 +159,21 @@ def tile_picked_codelapminmx_none_p_kernel(
             )
 
         steps = [(c, t) for c in range(2) for t in range(TILES)]
-        for i, step in enumerate(steps):
+        first_neighbour(*steps[0])
+        w2_scales = keep.tile([P, H], U8, name="w2_scales", align_bytes=64)
+        nc.vector.tensor_copy(
+            w2_scales[:].bitcast(I32).rearrange("p (t a v) -> p a t v", t=4, v=2),
+            w2_bytes_picked[:].bitcast(I32).rearrange("p (a t v) -> p a t v", t=4, v=2),
+        )
+        lift_odd_rows(w2_scales)
+        for before, step in zip(steps, steps[1:]):
             first_neighbour(*step)
-            if i > 0:
-                second_neighbour(*steps[i - 1])
+            second_neighbour(*before)
         second_neighbour(*steps[-1])
-        quantise(0)
 
         w2_words_picked = keep.tile([P, H], U32, name="w2_words_picked", tag="shared", align_bytes=64)
         nc.vector.tensor_copy(w2_words_picked[:], d_table[:].indirect(k2_list[:]))
+        quantise(0)
         w2_words = keep.tile([P, H], U32, name="w2_words", align_bytes=64)
         nc.vector.tensor_copy(
             w2_words[:].rearrange("p (t a v) -> p a t v", t=4, v=8),
@@ -187,13 +187,30 @@ def tile_picked_codelapminmx_none_p_kernel(
             for i, (c0, c1) in enumerate(spans):
                 acc = product("bank%d_%d" % (t, i), w2_words, w2_scales, t, z_words, z_scales, c0, c1)
                 nc.scalar.activation(wide[t][:, c0:c1], acc[:], COPY, scale=0.0625)
-        for t in range(TILES):
-            third = keep.tile([P, S], F32, name="third%d" % t)
-            fourth = keep.tile([P, S], F32, name="fourth%d" % t)
-            larger = keep.tile([P, S], F32, name="larger%d" % t)
-            result = keep.tile([P, S], F32, name="result%d" % t)
-            nc.vector.tensor_copy(third[:], wide[t][:].indirect(n3_list[:]))
-            nc.vector.tensor_copy(fourth[:], wide[t][:].indirect(n4_list[:]))
-            nc.vector.tensor_tensor(larger[:], third[:], wide[t][:, :S], ALU.max)
-            nc.vector.tensor_tensor(result[:], larger[:], fourth[:], ALU.min)
-            nc.sync.dma_start(out_rows[t], result[:])
+        third = [keep.tile([P, S], F32, name="third%d" % t) for t in range(TILES)]
+        fourth = [keep.tile([P, S], F32, name="fourth%d" % t) for t in range(TILES)]
+        larger = [keep.tile([P, S], F32, name="larger%d" % t) for t in range(TILES)]
+        result = [keep.tile([P, S], F32, name="result%d" % t) for t in range(TILES)]
+
+        def fetch(dst, t, offsets, c0, c1):
+            nc.vector.tensor_copy(dst[t][:, c0:c1], wide[t][:].indirect(offsets[:, c0 // 16 : c1 // 16]))
+
+        def take_larger(t):
+            nc.vector.tensor_tensor(larger[t][:], third[t][:], wide[t][:, :S], ALU.max)
+
+        def finish(t, c0, c1, queue):
+            nc.vector.tensor_tensor(result[t][:, c0:c1], larger[t][:, c0:c1], fourth[t][:, c0:c1], ALU.min)
+            queue.dma_start(out_rows[t][:, :, c0:c1], result[t][:, c0:c1])
+
+        last = TILES - 1
+        fetch(third, 0, n3_list, 0, S)
+        for t in range(last):
+            fetch(fourth, t, n4_list, 0, S)
+            take_larger(t)
+            fetch(third, t + 1, n3_list, 0, S)
+            finish(t, 0, S, nc.sync)
+        take_larger(last)
+        fetch(fourth, last, n4_list, 0, HALF)
+        fetch(fourth, last, n4_list, HALF, S)
+        finish(last, 0, HALF, nc.sync)
+        finish(last, HALF, S, nc.scalar)

@@ -1,6 +1,7 @@
 from contextlib import ExitStack
 
 import concourse.mybir as mybir
+from concourse.masks import make_identity
 
 F32 = mybir.dt.float32
 BF16 = mybir.dt.bfloat16
@@ -11,6 +12,7 @@ U8 = mybir.dt.uint8
 FP8X4 = mybir.dt.float8_e4m3fn_x4
 ALU = mybir.AluOpType
 COPY = mybir.ActivationFunctionType.Copy
+RELU = mybir.ActivationFunctionType.Relu
 
 P = 128
 K, T, S, G, H = 512, 1024, 512, 2048, 512
@@ -43,14 +45,14 @@ def tile_picked_codelapminmx_none_p_kernel(
         k1_list = load_list("k1_list", k1)
         d_rows = d_scales[0].bitcast(I32)
         d_source = d_words[0].rearrange("p n t -> p (n t)").bitcast(I32)
-        nc.sync.dma_start(d_table[:].bitcast(I32)[:, : G // 4], d_source[:, : G // 4])
+        nc.sync.dma_start(d_table[:].bitcast(I32)[:, : G // 8], d_source[:, : G // 8])
         for e in range(2):
             nc.sync.dma_start(d_bytes[:].bitcast(I32)[e:P:16, :], d_rows[e:16:2, :])
         x_rows = x_scales[0].bitcast(I32)
         for j in range(4):
             nc.sync.dma_start(x_bytes[:].bitcast(I32)[j:P:32, :], x_rows[j:16:4, :])
         offs_list = load_list("offs_list", offs)
-        nc.sync.dma_start(d_table[:].bitcast(I32)[:, G // 4 :], d_source[:, G // 4 :])
+        nc.sync.dma_start(d_table[:].bitcast(I32)[:, G // 8 :], d_source[:, G // 8 :])
         nc.sync.dma_start(x_table[:].bitcast(I32), x_words[0].rearrange("p n t -> p (n t)").bitcast(I32))
         k2_list = load_list("k2_list", k2)
         n1_list = load_list("n1_list", n1)
@@ -60,6 +62,8 @@ def tile_picked_codelapminmx_none_p_kernel(
 
         gain = keep.tile([P, TILES], F32, name="gain")
         nc.gpsimd.dma_start(gain[:], gs.rearrange("(p t) o -> p (t o)", t=TILES))
+        identity = keep.tile([P, P], F32, name="identity")
+        make_identity(nc, identity[:])
         gain_self = keep.tile([P, TILES], F32, name="gain_self")
         gain_near = keep.tile([P, TILES], F32, name="gain_near")
         nc.scalar.activation(gain_self[:], gain[:], COPY, scale=0.0625)
@@ -82,7 +86,7 @@ def tile_picked_codelapminmx_none_p_kernel(
         )
         lift_odd_rows(w1_scales)
 
-        w1_words_picked = keep.tile([P, H], U32, name="w1_words_picked", align_bytes=64)
+        w1_words_picked = keep.tile([P, H], U32, name="w1_words_picked", tag="picked", align_bytes=64)
         nc.vector.tensor_copy(w1_words_picked[:], d_table[:].indirect(k1_list[:]))
 
         xq_words = keep.tile([P, S], U32, name="xq_words", align_bytes=64)
@@ -94,7 +98,7 @@ def tile_picked_codelapminmx_none_p_kernel(
         )
         nc.vector.tensor_copy(xq_words[:, HALF:], x_table[:].indirect(offs_list[:, 16:]))
 
-        w2_bytes_picked = keep.tile([P, H], U8, name="w2_bytes_picked", align_bytes=64)
+        w2_bytes_picked = keep.tile([P, H], U8, name="w2_bytes_picked", tag="picked", align_bytes=64)
         nc.vector.tensor_copy(w2_bytes_picked[:], d_bytes[:].indirect(k2_list[:]))
 
         def product(tag, words, scales, t, rhs_words, rhs_scales, c0, c1):
@@ -112,28 +116,21 @@ def tile_picked_codelapminmx_none_p_kernel(
 
         near = [keep.tile([P, S], F32, name="near%d" % t) for t in range(TILES)]
         wide = [keep.tile([P, 2 * S], F32, name="wide%d" % t) for t in range(TILES)]
-        late = []
         for t in range(TILES):
             spans = [(0, HALF), (HALF, S)] if t == 0 else [(0, S)]
             for i, (c0, c1) in enumerate(spans):
                 acc = product("bank%d_%d" % (t, i), w1_words, w1_scales, t, xq_words, xq_scales, c0, c1)
+                nc.scalar.activation(wide[t][:, S + c0 : S + c1], acc[:], COPY, scale=gain_self[:, t : t + 1])
                 nc.scalar.activation(near[t][:, c0:c1], acc[:], COPY, scale=gain_near[:, t : t + 1])
-                if c0 == 0:
-                    nc.scalar.activation(wide[t][:, S : S + HALF], acc[:, :HALF], COPY, scale=gain_self[:, t : t + 1])
-                if c1 == S:
-                    late.append((t, acc, HALF - c0))
-        for t, acc, c0 in late:
-            nc.scalar.activation(wide[t][:, S + HALF :], acc[:, c0 : c0 + HALF], COPY, scale=gain_self[:, t : t + 1])
 
         z_words = keep.tile([P, S], U32, name="z_words", align_bytes=64)
         z_scales = keep.tile([P, S], U8, name="z_scales", align_bytes=64)
-        z = [keep.tile([P, TILES, HALF], F32, name="z%d" % c) for c in range(2)]
+        z = [keep.tile([P, TILES, HALF], F32, name="z0")]
         grouped = [keep.tile([P, HALF, TILES], BF16, name="grouped%d" % c, align_bytes=64) for c in range(2)]
         partial = {}
 
         def first_neighbour(c, t):
-            tag = "shared" if (c, t) == (0, TILES - 1) else "partial%d_%d" % (c, t)
-            partial[c, t] = keep.tile([P, HALF], F32, name="partial%d_%d" % (c, t), tag=tag, align_bytes=64)
+            partial[c, t] = keep.tile([P, HALF], F32, name="partial%d_%d" % (c, t), align_bytes=64)
             nc.vector.tensor_tensor(
                 partial[c, t][:],
                 near[t][:].indirect(n1_list[:, c * 16 : (c + 1) * 16]),
@@ -158,59 +155,87 @@ def tile_picked_codelapminmx_none_p_kernel(
                 in_=grouped[c][:].rearrange("p s t -> p (s t)"),
             )
 
-        steps = [(c, t) for c in range(2) for t in range(TILES)]
-        first_neighbour(*steps[0])
+        for t in range(TILES):
+            first_neighbour(0, t)
+            first_neighbour(1, t)
+            second_neighbour(0, t)
         w2_scales = keep.tile([P, H], U8, name="w2_scales", align_bytes=64)
         nc.vector.tensor_copy(
             w2_scales[:].bitcast(I32).rearrange("p (t a v) -> p a t v", t=4, v=2),
             w2_bytes_picked[:].bitcast(I32).rearrange("p (a t v) -> p a t v", t=4, v=2),
         )
         lift_odd_rows(w2_scales)
-        for before, step in zip(steps, steps[1:]):
-            first_neighbour(*step)
-            second_neighbour(*before)
-        second_neighbour(*steps[-1])
+        z.append(keep.tile([P, TILES, HALF], F32, name="z1", tag="partial0_3", align_bytes=64))
+        for t in range(TILES):
+            second_neighbour(1, t)
 
-        w2_words_picked = keep.tile([P, H], U32, name="w2_words_picked", tag="shared", align_bytes=64)
+        w2_words_picked = keep.tile([P, H], U32, name="w2_words_picked", tag="partial1_2", align_bytes=64)
         nc.vector.tensor_copy(w2_words_picked[:], d_table[:].indirect(k2_list[:]))
         quantise(0)
         w2_words = keep.tile([P, H], U32, name="w2_words", align_bytes=64)
-        nc.vector.tensor_copy(
-            w2_words[:].rearrange("p (t a v) -> p a t v", t=4, v=8),
-            w2_words_picked[:].rearrange("p (a t v) -> p a t v", t=4, v=8),
-        )
+        dealt = w2_words[:].rearrange("p (t a v) -> p a t v", t=4, v=8)
+        undealt = w2_words_picked[:].rearrange("p (a t v) -> p a t v", t=4, v=8)
+        nc.vector.tensor_copy(dealt[:, :, :1, :], undealt[:, :, :1, :])
         quantise(1)
+        nc.vector.tensor_copy(dealt[:, :, 1:, :], undealt[:, :, 1:, :])
 
+        last = TILES - 1
+        own = [keep.tile([P, S], F32, name="own%d" % t) for t in range(last)]
         out_rows = out.rearrange("(a t v) s -> t a v s", t=TILES, v=8)
-        for t in range(TILES):
+
+        def second_product(t):
             spans = [(0, HALF), (HALF, S)] if t == 0 else [(0, S)]
             for i, (c0, c1) in enumerate(spans):
                 acc = product("bank%d_%d" % (t, i), w2_words, w2_scales, t, z_words, z_scales, c0, c1)
-                nc.scalar.activation(wide[t][:, c0:c1], acc[:], COPY, scale=0.0625)
+                copies = [wide[t], own[t]] if t == 0 else own[t : t + 1] + [wide[t]]
+                for target in copies:
+                    nc.scalar.activation(target[:, c0:c1], acc[:], COPY, scale=0.0625)
+
+        for t in range(last):
+            second_product(t)
+
         third = [keep.tile([P, S], F32, name="third%d" % t) for t in range(TILES)]
-        fourth = [keep.tile([P, S], F32, name="fourth%d" % t) for t in range(TILES)]
-        larger = [keep.tile([P, S], F32, name="larger%d" % t) for t in range(TILES)]
-        result = [keep.tile([P, S], F32, name="result%d" % t) for t in range(TILES)]
+        fourth = [keep.tile([P, S], F32, name="fourth%d" % t, tag="own2" if t == 1 else "fourth%d" % t) for t in range(TILES)]
+        result = [keep.tile([P, S], F32, name="result%d" % t) for t in range(last)]
+        larger = {}
 
         def fetch(dst, t, offsets, c0, c1):
             nc.vector.tensor_copy(dst[t][:, c0:c1], wide[t][:].indirect(offsets[:, c0 // 16 : c1 // 16]))
 
-        def take_larger(t):
-            nc.vector.tensor_tensor(larger[t][:], third[t][:], wide[t][:, :S], ALU.max)
+        def larger_by_sum(t):
+            nc.vector.tensor_tensor(third[t][:], wide[t][:].indirect(n3_list[:]), own[t][:], ALU.subtract)
+            excess = keep.tile([P, S], F32, name="excess%d" % t)
+            nc.scalar.activation(excess[:], third[t][:], RELU)
+            summed = psum.tile([P, S], F32, name="summed%d" % t, tag="bank%d_0" % t)
+            for b in range(4):
+                block = slice(b * P, (b + 1) * P)
+                nc.tensor.matmul(summed[:, block], wide[t][:, block], identity[:], start=True, stop=False, is_transpose=True)
+                nc.tensor.matmul(summed[:, block], excess[:, block], identity[:], start=False, stop=True, is_transpose=True)
+            turned = keep.tile([P, S], F32, name="turned%d" % t)
+            nc.scalar.copy(turned[:], summed[:])
+            larger[t] = psum.tile([P, S], F32, name="larger%d" % t, tag="larger%d" % t)
+            for b in range(4):
+                block = slice(b * P, (b + 1) * P)
+                nc.tensor.transpose(larger[t][:, block], turned[:, block], identity[:])
 
         def finish(t, c0, c1, queue):
             nc.vector.tensor_tensor(result[t][:, c0:c1], larger[t][:, c0:c1], fourth[t][:, c0:c1], ALU.min)
             queue.dma_start(out_rows[t][:, :, c0:c1], result[t][:, c0:c1])
 
-        last = TILES - 1
-        fetch(third, 0, n3_list, 0, S)
-        for t in range(last):
-            fetch(fourth, t, n4_list, 0, S)
-            take_larger(t)
-            fetch(third, t + 1, n3_list, 0, S)
-            finish(t, 0, S, nc.sync)
-        take_larger(last)
-        fetch(fourth, last, n4_list, 0, HALF)
-        fetch(fourth, last, n4_list, HALF, S)
-        finish(last, 0, HALF, nc.sync)
-        finish(last, HALF, S, nc.scalar)
+        fetch(fourth, 0, n4_list, 0, S)
+        larger_by_sum(0)
+        second_product(last)
+        larger_by_sum(1)
+        larger_by_sum(2)
+        fetch(fourth, 2, n4_list, 0, S)
+        fetch(fourth, 1, n4_list, 0, S)
+        fetch(third, last, n3_list, 0, S)
+        fetch(fourth, last, n4_list, 0, S)
+        larger[last] = keep.tile([P, S], F32, name="larger_last")
+        nc.vector.tensor_tensor(larger[last][:], third[last][:], wide[last][:, :S], ALU.max)
+        result.append(keep.tile([P, S], F32, name="result_last", tag="turned0"))
+        finish(0, 0, S, nc.sync)
+        finish(last, 0, S, nc.sync)
+        finish(1, 0, S, nc.sync)
+        finish(2, 0, HALF, nc.sync)
+        finish(2, HALF, S, nc.scalar)

@@ -1,7 +1,6 @@
 from contextlib import ExitStack
 
 import concourse.mybir as mybir
-from concourse.masks import make_identity
 
 F32 = mybir.dt.float32
 BF16 = mybir.dt.bfloat16
@@ -16,8 +15,16 @@ RELU = mybir.ActivationFunctionType.Relu
 
 P = 128
 K, T, S, G, H = 512, 1024, 512, 2048, 512
-TILES = 4
+TILES = H // P
+LAST = TILES - 1
 HALF = S // 2
+GROUP = 16
+QUADRANT = 32
+SCALE_ROWS = K // 32
+ROWS_TOGETHER = 8
+LEAD = G // 8
+ON_GPSIMD = 2
+SIXTEENTH = 0.0625
 FLOPS = 2 * 2 * K * H * S
 
 
@@ -31,9 +38,12 @@ def tile_picked_codelapminmx_none_p_kernel(
         psum = ctx.enter_context(tc.psum_pool(name="psum", bufs=1))
 
         def load_list(name, dram):
-            tile = lists.tile([P, S // 16], U16, name=name)
+            tile = lists.tile([P, S // GROUP], U16, name=name)
             nc.sync.dma_start(tile[:], dram)
             return tile
+
+        def entries(offsets, c0, c1):
+            return offsets[:, c0 // GROUP : c1 // GROUP]
 
         d_bytes = keep.tile([P, G], U8, name="d_bytes", align_bytes=64)
         x_bytes = keep.tile([P, T], U8, name="x_bytes", align_bytes=64)
@@ -45,14 +55,14 @@ def tile_picked_codelapminmx_none_p_kernel(
         k1_list = load_list("k1_list", k1)
         d_rows = d_scales[0].bitcast(I32)
         d_source = d_words[0].rearrange("p n t -> p (n t)").bitcast(I32)
-        nc.sync.dma_start(d_table[:].bitcast(I32)[:, : G // 8], d_source[:, : G // 8])
+        nc.sync.dma_start(d_table[:].bitcast(I32)[:, :LEAD], d_source[:, :LEAD])
         for e in range(2):
-            nc.sync.dma_start(d_bytes[:].bitcast(I32)[e:P:16, :], d_rows[e:16:2, :])
+            nc.sync.dma_start(d_bytes[:].bitcast(I32)[e:P:GROUP, :], d_rows[e:SCALE_ROWS:2, :])
         x_rows = x_scales[0].bitcast(I32)
         for j in range(4):
-            nc.sync.dma_start(x_bytes[:].bitcast(I32)[j:P:32, :], x_rows[j:16:4, :])
+            nc.sync.dma_start(x_bytes[:].bitcast(I32)[j:P:QUADRANT, :], x_rows[j:SCALE_ROWS:4, :])
         offs_list = load_list("offs_list", offs)
-        nc.sync.dma_start(d_table[:].bitcast(I32)[:, G // 8 :], d_source[:, G // 8 :])
+        nc.sync.dma_start(d_table[:].bitcast(I32)[:, LEAD:], d_source[:, LEAD:])
         nc.sync.dma_start(x_table[:].bitcast(I32), x_words[0].rearrange("p n t -> p (n t)").bitcast(I32))
         k2_list = load_list("k2_list", k2)
         n1_list = load_list("n1_list", n1)
@@ -62,47 +72,46 @@ def tile_picked_codelapminmx_none_p_kernel(
 
         gain = keep.tile([P, TILES], F32, name="gain")
         nc.gpsimd.dma_start(gain[:], gs.rearrange("(p t) o -> p (t o)", t=TILES))
-        identity = keep.tile([P, P], F32, name="identity")
-        make_identity(nc, identity[:])
         gain_self = keep.tile([P, TILES], F32, name="gain_self")
         gain_near = keep.tile([P, TILES], F32, name="gain_near")
-        nc.scalar.activation(gain_self[:], gain[:], COPY, scale=0.0625)
-        nc.scalar.activation(gain_near[:], gain[:], COPY, scale=0.0625 * 0.75)
+        nc.scalar.activation(gain_self[:], gain[:], COPY, scale=SIXTEENTH)
+        nc.scalar.activation(gain_near[:], gain[:], COPY, scale=SIXTEENTH * 0.75)
 
-        def lift_odd_rows(plane):
-            rows = plane[:].bitcast(I32)
+        def lift_odd_rows(scales):
+            rows = scales[:].bitcast(I32)
             for e in range(2):
-                nc.sync.dma_start(rows[2 + e : P : 32, :], rows[16 + e : P : 32, :])
+                nc.sync.dma_start(rows[2 + e : P : QUADRANT, :], rows[GROUP + e : P : QUADRANT, :])
 
         w1_bytes_picked = keep.tile([P, H], U8, name="w1_bytes_picked", align_bytes=64)
         nc.vector.tensor_copy(w1_bytes_picked[:], d_bytes[:].indirect(k1_list[:]))
-
         xq_scales = keep.tile([P, S], U8, name="xq_scales", align_bytes=64)
         nc.vector.tensor_copy(xq_scales[:], x_bytes[:].indirect(offs_list[:]))
         w1_scales = keep.tile([P, H], U8, name="w1_scales", align_bytes=64)
         nc.vector.tensor_copy(
-            w1_scales[:].rearrange("p (t c i) -> p c t i", t=4, i=16),
-            w1_bytes_picked[:].rearrange("p (c i t) -> p c t i", t=4, i=16),
+            w1_scales[:].rearrange("p (t c i) -> p c t i", t=TILES, i=16),
+            w1_bytes_picked[:].rearrange("p (c i t) -> p c t i", t=TILES, i=16),
         )
         lift_odd_rows(w1_scales)
 
         w1_words_picked = keep.tile([P, H], U32, name="w1_words_picked", tag="picked", align_bytes=64)
         nc.vector.tensor_copy(w1_words_picked[:], d_table[:].indirect(k1_list[:]))
-
         xq_words = keep.tile([P, S], U32, name="xq_words", align_bytes=64)
-        nc.vector.tensor_copy(xq_words[:, :HALF], x_table[:].indirect(offs_list[:, :16]))
+        nc.vector.tensor_copy(xq_words[:, :HALF], x_table[:].indirect(entries(offs_list, 0, HALF)))
         w1_words = keep.tile([P, H], U32, name="w1_words", align_bytes=64)
         nc.vector.tensor_copy(
-            w1_words[:].rearrange("p (t c i) -> p c t i", t=4, i=4),
-            w1_words_picked[:].rearrange("p (c i t) -> p c t i", t=4, i=4),
+            w1_words[:].rearrange("p (t c i) -> p c t i", t=TILES, i=4),
+            w1_words_picked[:].rearrange("p (c i t) -> p c t i", t=TILES, i=4),
         )
-        nc.vector.tensor_copy(xq_words[:, HALF:], x_table[:].indirect(offs_list[:, 16:]))
+        nc.vector.tensor_copy(xq_words[:, HALF:], x_table[:].indirect(entries(offs_list, HALF, S)))
 
         w2_bytes_picked = keep.tile([P, H], U8, name="w2_bytes_picked", tag="picked", align_bytes=64)
         nc.vector.tensor_copy(w2_bytes_picked[:], d_bytes[:].indirect(k2_list[:]))
 
-        def product(tag, words, scales, t, rhs_words, rhs_scales, c0, c1):
-            acc = psum.tile([P, c1 - c0], F32, name=tag, tag=tag)
+        def spans(t):
+            return [(0, HALF), (HALF, S)] if t == 0 else [(0, S)]
+
+        def product(words, scales, t, rhs_words, rhs_scales, c0, c1):
+            acc = psum.tile([P, c1 - c0], F32, name="bank%d_%d" % (t, c0 // HALF))
             nc.tensor.matmul_mx(
                 out=acc[:],
                 lhsT=words[:, t * P : (t + 1) * P].bitcast(FP8X4),
@@ -117,125 +126,116 @@ def tile_picked_codelapminmx_none_p_kernel(
         near = [keep.tile([P, S], F32, name="near%d" % t) for t in range(TILES)]
         wide = [keep.tile([P, 2 * S], F32, name="wide%d" % t) for t in range(TILES)]
         for t in range(TILES):
-            spans = [(0, HALF), (HALF, S)] if t == 0 else [(0, S)]
-            for i, (c0, c1) in enumerate(spans):
-                acc = product("bank%d_%d" % (t, i), w1_words, w1_scales, t, xq_words, xq_scales, c0, c1)
+            for c0, c1 in spans(t):
+                acc = product(w1_words, w1_scales, t, xq_words, xq_scales, c0, c1)
                 nc.scalar.activation(wide[t][:, S + c0 : S + c1], acc[:], COPY, scale=gain_self[:, t : t + 1])
                 nc.scalar.activation(near[t][:, c0:c1], acc[:], COPY, scale=gain_near[:, t : t + 1])
 
         z_words = keep.tile([P, S], U32, name="z_words", align_bytes=64)
         z_scales = keep.tile([P, S], U8, name="z_scales", align_bytes=64)
         z = [keep.tile([P, TILES, HALF], F32, name="z0")]
-        grouped = [keep.tile([P, HALF, TILES], BF16, name="grouped%d" % c, align_bytes=64) for c in range(2)]
+        grouped = [keep.tile([P, HALF, TILES], BF16, name="grouped%d" % half, align_bytes=64) for half in range(2)]
         partial = {}
 
-        def first_neighbour(c, t):
-            partial[c, t] = keep.tile([P, HALF], F32, name="partial%d_%d" % (c, t), align_bytes=64)
+        def first_neighbour(half, t):
+            c0, c1 = half * HALF, (half + 1) * HALF
+            partial[half, t] = keep.tile([P, HALF], F32, name="partial%d_%d" % (half, t), align_bytes=64)
             nc.vector.tensor_tensor(
-                partial[c, t][:],
-                near[t][:].indirect(n1_list[:, c * 16 : (c + 1) * 16]),
-                wide[t][:, S + c * HALF : S + (c + 1) * HALF],
+                partial[half, t][:],
+                near[t][:].indirect(entries(n1_list, c0, c1)),
+                wide[t][:, S + c0 : S + c1],
                 ALU.subtract,
             )
 
-        def second_neighbour(c, t):
+        def second_neighbour(half, t):
+            c0, c1 = half * HALF, (half + 1) * HALF
             nc.vector.tensor_tensor(
-                z[c][:, t, :], near[t][:].indirect(n2_list[:, c * 16 : (c + 1) * 16]), partial[c, t][:], ALU.add
+                z[half][:, t, :], near[t][:].indirect(entries(n2_list, c0, c1)), partial[half, t][:], ALU.add
             )
-            if t == TILES - 1:
+            if t == LAST:
                 nc.scalar.copy(
-                    grouped[c][:].rearrange("p (b i) t -> p b t i", i=4),
-                    z[c][:].rearrange("p t (b i) -> p b t i", i=4),
+                    grouped[half][:].rearrange("p (b i) t -> p b t i", i=4),
+                    z[half][:].rearrange("p t (b i) -> p b t i", i=4),
                 )
 
-        def quantise(c):
+        def quantise(half):
             nc.vector.quantize_mx(
-                out=z_words[:, c * HALF : (c + 1) * HALF].bitcast(FP8X4),
-                scales=z_scales[:, c * HALF : (c + 1) * HALF],
-                in_=grouped[c][:].rearrange("p s t -> p (s t)"),
+                out=z_words[:, half * HALF : (half + 1) * HALF].bitcast(FP8X4),
+                scales=z_scales[:, half * HALF : (half + 1) * HALF],
+                in_=grouped[half][:].rearrange("p s t -> p (s t)"),
             )
 
         for t in range(TILES):
             first_neighbour(0, t)
             first_neighbour(1, t)
             second_neighbour(0, t)
+
         w2_scales = keep.tile([P, H], U8, name="w2_scales", align_bytes=64)
         nc.vector.tensor_copy(
-            w2_scales[:].bitcast(I32).rearrange("p (t a v) -> p a t v", t=4, v=2),
-            w2_bytes_picked[:].bitcast(I32).rearrange("p (a t v) -> p a t v", t=4, v=2),
+            w2_scales[:].bitcast(I32).rearrange("p (t a v) -> p a t v", t=TILES, v=ROWS_TOGETHER // 4),
+            w2_bytes_picked[:].bitcast(I32).rearrange("p (a t v) -> p a t v", t=TILES, v=ROWS_TOGETHER // 4),
         )
         lift_odd_rows(w2_scales)
-        z.append(keep.tile([P, TILES, HALF], F32, name="z1", tag="partial0_3", align_bytes=64))
+
+        z.append(keep.tile([P, TILES, HALF], F32, name="z1", tag="partial0_%d" % LAST, align_bytes=64))
         for t in range(TILES):
             second_neighbour(1, t)
 
-        w2_words_picked = keep.tile([P, H], U32, name="w2_words_picked", tag="partial1_2", align_bytes=64)
+        w2_words_picked = keep.tile([P, H], U32, name="w2_words_picked", tag="partial1_%d" % (LAST - 1), align_bytes=64)
         nc.vector.tensor_copy(w2_words_picked[:], d_table[:].indirect(k2_list[:]))
         quantise(0)
         w2_words = keep.tile([P, H], U32, name="w2_words", align_bytes=64)
-        dealt = w2_words[:].rearrange("p (t a v) -> p a t v", t=4, v=8)
-        undealt = w2_words_picked[:].rearrange("p (a t v) -> p a t v", t=4, v=8)
+        dealt = w2_words[:].rearrange("p (t a v) -> p a t v", t=TILES, v=ROWS_TOGETHER)
+        undealt = w2_words_picked[:].rearrange("p (a t v) -> p a t v", t=TILES, v=ROWS_TOGETHER)
         nc.vector.tensor_copy(dealt[:, :, :1, :], undealt[:, :, :1, :])
         quantise(1)
         nc.vector.tensor_copy(dealt[:, :, 1:, :], undealt[:, :, 1:, :])
 
-        last = TILES - 1
-        own = [keep.tile([P, S], F32, name="own%d" % t) for t in range(last)]
-        out_rows = out.rearrange("(a t v) s -> t a v s", t=TILES, v=8)
-
-        def second_product(t):
-            spans = [(0, HALF), (HALF, S)] if t == 0 else [(0, S)]
-            for i, (c0, c1) in enumerate(spans):
-                acc = product("bank%d_%d" % (t, i), w2_words, w2_scales, t, z_words, z_scales, c0, c1)
-                copies = [wide[t], own[t]] if t == 0 else own[t : t + 1] + [wide[t]]
-                for target in copies:
-                    nc.scalar.activation(target[:, c0:c1], acc[:], COPY, scale=0.0625)
-
-        for t in range(last):
-            second_product(t)
+        out_rows = out.rearrange("(a t v) s -> t a v s", t=TILES, v=ROWS_TOGETHER)
+        banks = {}
+        for t in range(TILES):
+            for c0, c1 in spans(t):
+                banks[t, c0] = product(w2_words, w2_scales, t, z_words, z_scales, c0, c1)
+                nc.scalar.activation(wide[t][:, c0:c1], banks[t, c0][:], COPY, scale=SIXTEENTH)
 
         third = [keep.tile([P, S], F32, name="third%d" % t) for t in range(TILES)]
-        fourth = [keep.tile([P, S], F32, name="fourth%d" % t, tag="own2" if t == 1 else "fourth%d" % t) for t in range(TILES)]
-        result = [keep.tile([P, S], F32, name="result%d" % t) for t in range(last)]
-        larger = {}
+        fourth = [keep.tile([P, S], F32, name="fourth%d" % t) for t in range(TILES)]
+        larger = [keep.tile([P, S], F32, name="larger%d" % t) for t in range(TILES)]
+        result = [keep.tile([P, S], F32, name="result%d" % t) for t in range(TILES)]
 
         def fetch(dst, t, offsets, c0, c1):
-            nc.vector.tensor_copy(dst[t][:, c0:c1], wide[t][:].indirect(offsets[:, c0 // 16 : c1 // 16]))
+            nc.vector.tensor_copy(dst[t][:, c0:c1], wide[t][:].indirect(entries(offsets, c0, c1)))
 
-        def larger_by_sum(t):
-            nc.vector.tensor_tensor(third[t][:], wide[t][:].indirect(n3_list[:]), own[t][:], ALU.subtract)
+        def take_larger(t):
+            if t == 0:
+                nc.vector.tensor_tensor(larger[t][:], third[t][:], wide[t][:, :S], ALU.max)
+            else:
+                nc.vector.scalar_tensor_tensor(larger[t][:], banks[t, 0][:], SIXTEENTH, third[t][:], ALU.mult, ALU.max)
+
+        def smaller_by_difference(t):
+            above = keep.tile([P, S], F32, name="above%d" % t)
+            nc.gpsimd.tensor_tensor(above[:], larger[t][:], fourth[t][:], ALU.subtract)
             excess = keep.tile([P, S], F32, name="excess%d" % t)
-            nc.scalar.activation(excess[:], third[t][:], RELU)
-            summed = psum.tile([P, S], F32, name="summed%d" % t, tag="bank%d_0" % t)
-            for b in range(4):
-                block = slice(b * P, (b + 1) * P)
-                nc.tensor.matmul(summed[:, block], wide[t][:, block], identity[:], start=True, stop=False, is_transpose=True)
-                nc.tensor.matmul(summed[:, block], excess[:, block], identity[:], start=False, stop=True, is_transpose=True)
-            turned = keep.tile([P, S], F32, name="turned%d" % t)
-            nc.scalar.copy(turned[:], summed[:])
-            larger[t] = psum.tile([P, S], F32, name="larger%d" % t, tag="larger%d" % t)
-            for b in range(4):
-                block = slice(b * P, (b + 1) * P)
-                nc.tensor.transpose(larger[t][:, block], turned[:, block], identity[:])
+            nc.scalar.activation(excess[:], above[:], RELU)
+            nc.gpsimd.tensor_tensor(result[t][:], larger[t][:], excess[:], ALU.subtract)
+            nc.scalar.dma_start(out_rows[t], result[t][:])
 
-        def finish(t, c0, c1, queue):
+        def smaller(t, c0, c1):
             nc.vector.tensor_tensor(result[t][:, c0:c1], larger[t][:, c0:c1], fourth[t][:, c0:c1], ALU.min)
-            queue.dma_start(out_rows[t][:, :, c0:c1], result[t][:, c0:c1])
+            nc.sync.dma_start(out_rows[t][:, :, c0:c1], result[t][:, c0:c1])
 
-        fetch(fourth, 0, n4_list, 0, S)
-        larger_by_sum(0)
-        second_product(last)
-        larger_by_sum(1)
-        larger_by_sum(2)
-        fetch(fourth, 2, n4_list, 0, S)
-        fetch(fourth, 1, n4_list, 0, S)
-        fetch(third, last, n3_list, 0, S)
-        fetch(fourth, last, n4_list, 0, S)
-        larger[last] = keep.tile([P, S], F32, name="larger_last")
-        nc.vector.tensor_tensor(larger[last][:], third[last][:], wide[last][:, :S], ALU.max)
-        result.append(keep.tile([P, S], F32, name="result_last", tag="turned0"))
-        finish(0, 0, S, nc.sync)
-        finish(last, 0, S, nc.sync)
-        finish(1, 0, S, nc.sync)
-        finish(2, 0, HALF, nc.sync)
-        finish(2, HALF, S, nc.scalar)
+        for t in range(LAST):
+            fetch(third, t, n3_list, 0, S)
+            fetch(fourth, t, n4_list, 0, S)
+            take_larger(t)
+            if t < ON_GPSIMD:
+                smaller_by_difference(t)
+
+        fetch(third, LAST, n3_list, 0, S)
+        for t in range(ON_GPSIMD, LAST):
+            smaller(t, 0, S)
+        take_larger(LAST)
+        fetch(fourth, LAST, n4_list, 0, HALF)
+        fetch(fourth, LAST, n4_list, HALF, S)
+        smaller(LAST, 0, HALF)
+        smaller(LAST, HALF, S)

from contextlib import ExitStack

import concourse.mybir as mybir

F32 = mybir.dt.float32
BF16 = mybir.dt.bfloat16
I32 = mybir.dt.int32
U32 = mybir.dt.uint32
U16 = mybir.dt.uint16
U8 = mybir.dt.uint8
FP8X4 = mybir.dt.float8_e4m3fn_x4
ALU = mybir.AluOpType
COPY = mybir.ActivationFunctionType.Copy
RELU = mybir.ActivationFunctionType.Relu

P = 128
K, T, S, G, H = 512, 1024, 512, 2048, 512
TILES = H // P
LAST = TILES - 1
HALF = S // 2
GROUP = 16
QUADRANT = 32
SCALE_ROWS = K // 32
ROWS_TOGETHER = 8
LEAD = G // 8
ON_GPSIMD = 2
SIXTEENTH = 0.0625
FLOPS = 2 * 2 * K * H * S


def tile_picked_codelapminmx_none_p_kernel(
    tc, x_words, x_scales, d_words, d_scales, gs, offs, k1, n1, n2, k2, n3, n4, out
):
    nc = tc.nc
    with ExitStack() as ctx:
        lists = ctx.enter_context(tc.tile_pool(name="lists", bufs=1))
        keep = ctx.enter_context(tc.tile_pool(name="keep", bufs=1))
        psum = ctx.enter_context(tc.psum_pool(name="psum", bufs=1))

        def load_list(name, dram):
            tile = lists.tile([P, S // GROUP], U16, name=name)
            nc.sync.dma_start(tile[:], dram)
            return tile

        def entries(offsets, c0, c1):
            return offsets[:, c0 // GROUP : c1 // GROUP]

        d_bytes = keep.tile([P, G], U8, name="d_bytes", align_bytes=64)
        x_bytes = keep.tile([P, T], U8, name="x_bytes", align_bytes=64)
        d_table = keep.tile([P, G], U32, name="d_table", align_bytes=64)
        x_table = keep.tile([P, T], U32, name="x_table", align_bytes=64)
        nc.vector.memset(d_bytes[:].bitcast(I32), 0)
        nc.vector.memset(x_bytes[:].bitcast(I32), 0)

        k1_list = load_list("k1_list", k1)
        d_rows = d_scales[0].bitcast(I32)
        d_source = d_words[0].rearrange("p n t -> p (n t)").bitcast(I32)
        nc.sync.dma_start(d_table[:].bitcast(I32)[:, :LEAD], d_source[:, :LEAD])
        for e in range(2):
            nc.sync.dma_start(d_bytes[:].bitcast(I32)[e:P:GROUP, :], d_rows[e:SCALE_ROWS:2, :])
        x_rows = x_scales[0].bitcast(I32)
        for j in range(4):
            nc.sync.dma_start(x_bytes[:].bitcast(I32)[j:P:QUADRANT, :], x_rows[j:SCALE_ROWS:4, :])
        offs_list = load_list("offs_list", offs)
        nc.sync.dma_start(d_table[:].bitcast(I32)[:, LEAD:], d_source[:, LEAD:])
        nc.sync.dma_start(x_table[:].bitcast(I32), x_words[0].rearrange("p n t -> p (n t)").bitcast(I32))
        k2_list = load_list("k2_list", k2)
        n1_list = load_list("n1_list", n1)
        n2_list = load_list("n2_list", n2)
        n3_list = load_list("n3_list", n3)
        n4_list = load_list("n4_list", n4)

        gain = keep.tile([P, TILES], F32, name="gain")
        nc.gpsimd.dma_start(gain[:], gs.rearrange("(p t) o -> p (t o)", t=TILES))
        gain_self = keep.tile([P, TILES], F32, name="gain_self")
        gain_near = keep.tile([P, TILES], F32, name="gain_near")
        nc.scalar.activation(gain_self[:], gain[:], COPY, scale=SIXTEENTH)
        nc.scalar.activation(gain_near[:], gain[:], COPY, scale=SIXTEENTH * 0.75)

        def lift_odd_rows(scales):
            rows = scales[:].bitcast(I32)
            for e in range(2):
                nc.sync.dma_start(rows[2 + e : P : QUADRANT, :], rows[GROUP + e : P : QUADRANT, :])

        w1_bytes_picked = keep.tile([P, H], U8, name="w1_bytes_picked", align_bytes=64)
        nc.vector.tensor_copy(w1_bytes_picked[:], d_bytes[:].indirect(k1_list[:]))
        xq_scales = keep.tile([P, S], U8, name="xq_scales", align_bytes=64)
        nc.vector.tensor_copy(xq_scales[:], x_bytes[:].indirect(offs_list[:]))
        w1_scales = keep.tile([P, H], U8, name="w1_scales", align_bytes=64)
        nc.vector.tensor_copy(
            w1_scales[:].rearrange("p (t c i) -> p c t i", t=TILES, i=16),
            w1_bytes_picked[:].rearrange("p (c i t) -> p c t i", t=TILES, i=16),
        )
        lift_odd_rows(w1_scales)

        w1_words_picked = keep.tile([P, H], U32, name="w1_words_picked", tag="picked", align_bytes=64)
        nc.vector.tensor_copy(w1_words_picked[:], d_table[:].indirect(k1_list[:]))
        xq_words = keep.tile([P, S], U32, name="xq_words", align_bytes=64)
        nc.vector.tensor_copy(xq_words[:, :HALF], x_table[:].indirect(entries(offs_list, 0, HALF)))
        w1_words = keep.tile([P, H], U32, name="w1_words", align_bytes=64)
        nc.vector.tensor_copy(
            w1_words[:].rearrange("p (t c i) -> p c t i", t=TILES, i=4),
            w1_words_picked[:].rearrange("p (c i t) -> p c t i", t=TILES, i=4),
        )
        nc.vector.tensor_copy(xq_words[:, HALF:], x_table[:].indirect(entries(offs_list, HALF, S)))

        w2_bytes_picked = keep.tile([P, H], U8, name="w2_bytes_picked", tag="picked", align_bytes=64)
        nc.vector.tensor_copy(w2_bytes_picked[:], d_bytes[:].indirect(k2_list[:]))

        def spans(t):
            return [(0, HALF), (HALF, S)] if t == 0 else [(0, S)]

        def product(words, scales, t, rhs_words, rhs_scales, c0, c1):
            acc = psum.tile([P, c1 - c0], F32, name="bank%d_%d" % (t, c0 // HALF))
            nc.tensor.matmul_mx(
                out=acc[:],
                lhsT=words[:, t * P : (t + 1) * P].bitcast(FP8X4),
                lhsT_scale=scales[:, t * P : (t + 1) * P],
                rhs=rhs_words[:, c0:c1].bitcast(FP8X4),
                rhs_scale=rhs_scales[:, c0:c1],
                start=True,
                stop=True,
            )
            return acc

        near = [keep.tile([P, S], F32, name="near%d" % t) for t in range(TILES)]
        wide = [keep.tile([P, 2 * S], F32, name="wide%d" % t) for t in range(TILES)]
        for t in range(TILES):
            for c0, c1 in spans(t):
                acc = product(w1_words, w1_scales, t, xq_words, xq_scales, c0, c1)
                nc.scalar.activation(wide[t][:, S + c0 : S + c1], acc[:], COPY, scale=gain_self[:, t : t + 1])
                nc.scalar.activation(near[t][:, c0:c1], acc[:], COPY, scale=gain_near[:, t : t + 1])

        z_words = keep.tile([P, S], U32, name="z_words", align_bytes=64)
        z_scales = keep.tile([P, S], U8, name="z_scales", align_bytes=64)
        z = [keep.tile([P, TILES, HALF], F32, name="z0")]
        grouped = [keep.tile([P, HALF, TILES], BF16, name="grouped%d" % half, align_bytes=64) for half in range(2)]
        partial = {}

        def first_neighbour(half, t):
            c0, c1 = half * HALF, (half + 1) * HALF
            partial[half, t] = keep.tile([P, HALF], F32, name="partial%d_%d" % (half, t), align_bytes=64)
            nc.vector.tensor_tensor(
                partial[half, t][:],
                near[t][:].indirect(entries(n1_list, c0, c1)),
                wide[t][:, S + c0 : S + c1],
                ALU.subtract,
            )

        def second_neighbour(half, t):
            c0, c1 = half * HALF, (half + 1) * HALF
            nc.vector.tensor_tensor(
                z[half][:, t, :], near[t][:].indirect(entries(n2_list, c0, c1)), partial[half, t][:], ALU.add
            )
            if t == LAST:
                nc.scalar.copy(
                    grouped[half][:].rearrange("p (b i) t -> p b t i", i=4),
                    z[half][:].rearrange("p t (b i) -> p b t i", i=4),
                )

        def quantise(half):
            nc.vector.quantize_mx(
                out=z_words[:, half * HALF : (half + 1) * HALF].bitcast(FP8X4),
                scales=z_scales[:, half * HALF : (half + 1) * HALF],
                in_=grouped[half][:].rearrange("p s t -> p (s t)"),
            )

        for t in range(TILES):
            first_neighbour(0, t)
            first_neighbour(1, t)
            second_neighbour(0, t)

        w2_scales = keep.tile([P, H], U8, name="w2_scales", align_bytes=64)
        nc.vector.tensor_copy(
            w2_scales[:].bitcast(I32).rearrange("p (t a v) -> p a t v", t=TILES, v=ROWS_TOGETHER // 4),
            w2_bytes_picked[:].bitcast(I32).rearrange("p (a t v) -> p a t v", t=TILES, v=ROWS_TOGETHER // 4),
        )
        lift_odd_rows(w2_scales)

        z.append(keep.tile([P, TILES, HALF], F32, name="z1", tag="partial0_%d" % LAST, align_bytes=64))
        for t in range(TILES):
            second_neighbour(1, t)

        w2_words_picked = keep.tile([P, H], U32, name="w2_words_picked", tag="partial1_%d" % (LAST - 1), align_bytes=64)
        nc.vector.tensor_copy(w2_words_picked[:], d_table[:].indirect(k2_list[:]))
        quantise(0)
        w2_words = keep.tile([P, H], U32, name="w2_words", align_bytes=64)
        dealt = w2_words[:].rearrange("p (t a v) -> p a t v", t=TILES, v=ROWS_TOGETHER)
        undealt = w2_words_picked[:].rearrange("p (a t v) -> p a t v", t=TILES, v=ROWS_TOGETHER)
        nc.vector.tensor_copy(dealt[:, :, :1, :], undealt[:, :, :1, :])
        quantise(1)
        nc.vector.tensor_copy(dealt[:, :, 1:, :], undealt[:, :, 1:, :])

        out_rows = out.rearrange("(a t v) s -> t a v s", t=TILES, v=ROWS_TOGETHER)
        banks = {}
        for t in range(TILES):
            for c0, c1 in spans(t):
                banks[t, c0] = product(w2_words, w2_scales, t, z_words, z_scales, c0, c1)
                nc.scalar.activation(wide[t][:, c0:c1], banks[t, c0][:], COPY, scale=SIXTEENTH)

        third = [keep.tile([P, S], F32, name="third%d" % t) for t in range(TILES)]
        fourth = [keep.tile([P, S], F32, name="fourth%d" % t) for t in range(TILES)]
        larger = [keep.tile([P, S], F32, name="larger%d" % t) for t in range(TILES)]
        result = [keep.tile([P, S], F32, name="result%d" % t) for t in range(TILES)]

        def fetch(dst, t, offsets, c0, c1):
            nc.vector.tensor_copy(dst[t][:, c0:c1], wide[t][:].indirect(entries(offsets, c0, c1)))

        def take_larger(t):
            if t == 0:
                nc.vector.tensor_tensor(larger[t][:], third[t][:], wide[t][:, :S], ALU.max)
            else:
                nc.vector.scalar_tensor_tensor(larger[t][:], banks[t, 0][:], SIXTEENTH, third[t][:], ALU.mult, ALU.max)

        def smaller_by_difference(t):
            above = keep.tile([P, S], F32, name="above%d" % t)
            nc.gpsimd.tensor_tensor(above[:], larger[t][:], fourth[t][:], ALU.subtract)
            excess = keep.tile([P, S], F32, name="excess%d" % t)
            nc.scalar.activation(excess[:], above[:], RELU)
            nc.gpsimd.tensor_tensor(result[t][:], larger[t][:], excess[:], ALU.subtract)
            nc.scalar.dma_start(out_rows[t], result[t][:])

        def smaller(t, c0, c1):
            nc.vector.tensor_tensor(result[t][:, c0:c1], larger[t][:, c0:c1], fourth[t][:, c0:c1], ALU.min)
            nc.sync.dma_start(out_rows[t][:, :, c0:c1], result[t][:, c0:c1])

        for t in range(LAST):
            fetch(third, t, n3_list, 0, S)
            fetch(fourth, t, n4_list, 0, S)
            take_larger(t)
            if t < ON_GPSIMD:
                smaller_by_difference(t)

        fetch(third, LAST, n3_list, 0, S)
        for t in range(ON_GPSIMD, LAST):
            smaller(t, 0, S)
        take_larger(LAST)
        fetch(fourth, LAST, n4_list, 0, HALF)
        fetch(fourth, LAST, n4_list, HALF, S)
        smaller(LAST, 0, HALF)
        smaller(LAST, HALF, S)
